import numpy as np, ml_dtypes
CORES = [48,51,52,55]
N = 4
BF = ml_dtypes.bfloat16
W, H, P, RO, ST, TH = 4096, 2048, 256, 5, 1, 36
def place(o, i):
    return o[np.arange(8)[None, :, None, None], i]
def ground(rng):
    o = np.argsort(rng.random((8, W)), axis=-1); x = np.zeros((N, 8, 16, W), np.int64); top = np.zeros(8, np.int64)
    for g in range(8):
        m = int(rng.choice(np.array([3, 5, 8]))); c = rng.integers(0, 16, (m, 16)); s = np.linspace(0, m, W, endpoint=False)
        i = np.minimum(s.astype(np.int64), m - 1); f = (s - i)[:, None]
        b = np.rint(c[i] * (1 - f) + c[(i + 1) % m] * f).astype(np.int64).T
        y = b[None] + rng.integers(-1, 2, (N, 16, W))
        y = np.where(rng.random((N, 1, W)) < 0.03, rng.integers(0, 16, (N, 16, W)), y)
        x[:, g] = np.clip(y, 0, 15)[:, :, np.argsort(o[g])]; top[g] = W * 28 // (85 * m)
    return o, top, x
def knot(rng, r, share):
    k = (N, 8, 1, r.shape[3]); p = rng.integers(0, 15, k); q = np.minimum(p + rng.integers(1, 5, k), 15)
    hit = (rng.random(k) < share) & (np.arange(16)[None, None, :, None] == q)
    return np.where(hit, np.take_along_axis(r, p, 2), r)
def walk(rng, o, top, n):
    st = np.floor((rng.random((N, 8, 15, n)) * 1.2 - 0.2) * top[None, :, None, None]).astype(np.int64)
    st = st + np.where(rng.random(st.shape) < 0.01, rng.integers(0, W, st.shape), 0)
    a = rng.integers(0, W, (N, 8, 1, n))
    return knot(rng, place(o, np.concatenate([a, a + np.add.accumulate(st, axis=2)], axis=2) % W), 0.4)
def ladder(rng, lev):
    pm = np.argsort(rng.random((8, 16)), axis=-1)
    return np.clip(lev[:, :, None, :] - 15 * pm[None, :, :, None], 0, 15)
def pack(x, c, r):
    return {"x": np.ascontiguousarray(x.reshape(N, 128, W)).astype(np.float32).astype(BF), "c0": np.ascontiguousarray(c.reshape(N, 128, H)).astype(np.int32),
            "r0": np.ascontiguousarray(r.reshape(N, 128, P)).astype(np.int32)}
def setup_inputs(rng):
    o, top, x = ground(rng)
    return pack(x, walk(rng, o, top, H), walk(rng, o, top, P))
def setup_inputs_ties(rng):
    o = np.argsort(rng.random((8, W)), axis=-1); cls = np.argsort(o, axis=-1) % 7
    cr = np.where(rng.random((N, 8, W)) < 0.04, rng.integers(0, 7, (N, 8, W)), cls[None])
    lev = np.array([0, 1, TH, TH + 1, 2 * TH, 2 * TH + 1, 3 * TH + 2])[cr]
    def some(n):
        i = rng.integers(0, 6, (N, 8, n)); rows = [i]
        for p in range(15):
            jump = rng.random((N, 8, n)) < 0.04
            d = np.where(jump, rng.choice(np.array([-3, 3]), (N, 8, n)), rng.choice(np.array([-2, -2, -1, 0, 1, 2, 2]), (N, 8, n)))
            i = np.clip(i + d, 0, 5 + jump.astype(np.int64)); rows.append(i)
        i = np.stack(rows, axis=2)
        return place(o, i + 7 * rng.integers(0, W // 7, i.shape))
    return pack(ladder(rng, lev), some(H), some(P))
def setup_inputs_clash(rng):
    hi = np.arange(W - 64, W); last6 = (hi[:, None] * hi[None, :]) % 64 == 63; over = last6 & (hi[:, None] * (hi[None, :] + 64) > 2 ** 24)
    hu, hv = np.nonzero(over if np.any(over) else last6)
    nm = rng.random((8, W)) < 0.5; a = rng.integers(1, H - 1, 8); row = np.arange(16)[None, :, None]
    r = np.zeros((N, 8, 16, P), np.int64); c = np.zeros((N, 8, 16, H), np.int64); lev = np.zeros((N, 8, W), np.int64)
    for g in range(8):
        sp = np.array([0, H - 1, int(a[g]), int(a[g]) + H]); nm[g, sp] = True
        apart = rng.permutation(H)[:P] + H * rng.integers(0, 2, P)
        if g == 4: nm[g, apart] = True
        if g == 5: nm[g, W - 64:] = True
        ne, fa = np.flatnonzero(nm[g]), np.flatnonzero(~nm[g])
        if g < 2: u, v = sp[2:], np.array([0, 0])
        elif g < 4: u, v = sp[:2], np.array([int(rng.choice(ne)), 0])
        elif g == 4: u, v = apart, np.zeros(P, np.int64)
        elif g == 5: u, v = hi[hu], hi[hv]
        else: u, v = rng.choice(ne, 8), rng.choice(ne, 8)
        i = rng.integers(0, len(u), (N, P)); k = rng.integers(0, 16, (N, P))
        if g == 4: i = np.argsort(rng.random((N, P)), axis=-1)
        if g == 1 or g == 4: k = rng.integers(0, 14, (N, P))
        if g == 0: k[0, :3] = 15; k[0, 3] = 5; k[1] = 15; k[1, P - 1] = 3
        k[2] = np.minimum(k[2], 14)
        at = np.where(k < 15, k, rng.integers(0, 15, (N, P)))
        y = np.where(row > k[:, None], rng.choice(fa, (N, 16, P)), rng.choice(ne, (N, 16, P)))
        y = np.where(row == at[:, None], u[i][:, None], y)
        y[:, 15] = np.where(k == 14, y[:, 15], v[i]); r[:, g] = y
        flip = rng.random((N, W)) < 0.02; flip[:, sp] = False; flip[:3] = False
        lev[:, g] = np.where(nm[g][None] ^ flip, 0, 150) + rng.integers(0, 6, (N, W))
        c[:, g] = np.where(rng.random((N, 1, H)) < 0.5, rng.choice(ne, (N, 16, H)), rng.integers(0, W, (N, 16, H)))
    return pack(ladder(rng, lev), c, r)
def setup_inputs_loops(rng):
    o, top, x = ground(rng); x[:, ::2] = rng.integers(0, 3, (N, 4, 16, W))
    e = np.argsort(o, axis=-1); b = 1 + 2 * int(rng.integers(0, 4)); z = int(rng.integers(0, N))
    x[:, b] = np.where(e[b] % 3 == 0, rng.integers(0, 3, (N, 16, W)), x[:, b])
    def tie(r):
        kd = rng.integers(0, 8, (N, 8, r.shape[3]))
        for p in range(1, 16):
            r[:, :, p] = np.where(kd == 1, r[:, :, 0], r[:, :, p])
            if p > 1: r[:, :, p] = np.where(kd == 7, r[:, :, p % 2], r[:, :, p])
        for m, dst, src in ((2, 15, 0), (3, 15, 14), (4, 5, 0), (4, 9, 0), (5, 4, 1), (5, 6, 2), (6, 12, 3), (6, 8, 5)):
            r[:, :, dst] = np.where(kd == m, r[:, :, src], r[:, :, dst])
        return r
    w = walk(rng, o, top, P); w[z, b] = o[b][e[b][w[z, b]] // 3 * 3]
    return pack(x, tie(walk(rng, o, top, H)), tie(w))
def setup_inputs_calm(rng):
    o, top, x = ground(rng); q = rng.permutation(N)
    x[q[0]] = rng.integers(0, 3, (8, 16, W)); x[q[1]] = 15 * rng.integers(0, 2, (8, 16, W))
    x[:, int(rng.integers(0, 8))] = rng.integers(0, 3, (N, 16, W))
    e = np.argsort(o, axis=-1); home = e[None] % N == np.arange(N)[:, None, None]
    x = np.where(home[:, :, None], rng.integers(0, 3, x.shape), x)
    i = place(e, walk(rng, o, top, P)) // N * N + np.arange(N)[:, None, None, None]
    return pack(x, walk(rng, o, top, H), place(o, np.where(i < W, i, i - N)))
def setup_inputs_spread(rng):
    o = np.argsort(rng.random((8, W)), axis=-1); e = np.argsort(o, axis=-1) % 5
    x = np.floor(rng.random((N, 8, 16, W)) * np.exp2(4.0 - e)[None, :, None, :]).astype(np.int64)
    def some(n):
        k = rng.integers(0, 4, (N, 8, 1, n)); u = rng.random((N, 8, 16, n)); b = 5 * np.floor(u * (W // 5)).astype(np.int64)
        i = np.where(k == 0, np.floor(W * u).astype(np.int64), np.floor(W * u ** 4).astype(np.int64))
        i = np.where(k == 2, b + rng.integers(3, 5, u.shape), np.where(k == 3, b + rng.integers(2, 5, u.shape), i))
        return place(o, np.minimum(i, W - 1))
    return pack(x, some(H), some(P))
def check_inputs(d):
    bad = []; a = np.asarray(d["x"]).astype(np.float32)
    if not np.all((a >= 0) & (a <= 15) & (a == np.floor(a))): bad.append("whole numbers of x")
    for k in ("c0", "r0"):
        if np.min(d[k]) < 0 or np.max(d[k]) > W - 1: bad.append("range of " + k)
    return bad
def look(xs, R):
    return np.take_along_axis(xs, R.reshape(N, 8, 1, 16 * P), axis=3).reshape(N, 8, 16, 16, P)
def far(v, d):
    return np.add.reduce(np.abs(v[:, :, :, :16 - d] - v[:, :, :, d:]), axis=2)
def first(bad):
    return np.where(np.any(bad, axis=2), np.argmax(bad, axis=2), 15)[:, :, None, :]
def reference(x, c0, r0):
    xs = x.astype(np.float32).astype(np.int32).reshape(N, 8, 16, W); C = c0.astype(np.int64).reshape(N, 8, 16, H).copy()
    R = r0.astype(np.int64).reshape(N, 8, 16, P)
    kap = np.zeros(N, np.int64); row = np.arange(16)[None, None, :, None]
    for rnd in range(RO):
        if rnd > 0: R = np.roll(R, ST, axis=0)
        bad = far(look(xs, R), 1) > TH; fail = np.any(bad, axis=2); k = first(bad)
        rk = np.take_along_axis(R, k, 2)[:, :, 0]
        h = (((rk * R[:, :, 15]) >> 6) + rk + kap[:, None, None]) & (H - 1)
        R = np.where((row > k) & (row < 15), np.take_along_axis(C, h[:, :, None, :], 3), R)
        same = R[:, :, :, None] == R[:, :, None]
        q = 15 - np.argmax(same[:, :, :, ::-1], axis=3)
        p = first((q > row)[:, :, :15])
        R = np.where((row >= p) & (row <= np.take_along_axis(q, p, 2)), np.take_along_axis(R, p, 2), R)
        v = look(xs, R); k2 = first(far(v, 1) > TH)
        S = np.where((row > k2) & (row < 15), np.take_along_axis(R, k2, 2), R)
        for j in range(P - 1, -1, -1):
            a, g = np.nonzero(fail[:, :, j])
            C[a, g, :, h[a, g, j]] = S[:, :, :, j][a, g]
        near = far(v, 2) <= TH; R = R.copy()
        R[:, :, 1:14:2] = np.where(near[:, :, 0:13:2], R[:, :, 0:13:2], R[:, :, 1:14:2])
        kap = np.add.reduce(fail.astype(np.int64), axis=(1, 2))
    return {"yc": C.reshape(N, 128, H).astype(np.float32), "yr": R.reshape(N, 128, P).astype(np.float32)}

@@ -1,0 +1,475 @@
+from concourse.mybir import AluOpType, AxisListType, ActivationFunctionType
+
+OP = AluOpType
+ID = ActivationFunctionType.Identity
+ABS = ActivationFunctionType.Abs
+ROUNDS = 5
+TH = 36.0
+OFF = 2048.0
+NO = -8192.0
+CW = 2048 + 256
+NENG = 8
+BIG = float(2 ** 40)
+CFG = {"abs_a": True, "abs_b": False, "abs_2": True, "gv_a": 0, "gv_b": 0, "ch_a": 1, "ch_b": 1, "vf": 0.04, "wake": 0.08, "gam": 1.5}
+
+SCRATCH = {
+    "xw": ("sbuf", [128, 4096], "bfloat16"), "cw": ("sbuf", [128, CW], "float32"), "ci": ("sbuf", [128, 2048], "int32"),
+    "ri": ("sbuf", [128, 256], "int32"), "pint": ("sbuf", [128, 4], "int32"), "pf": ("sbuf", [128, 4], "float32"),
+    "icol2": ("sbuf", [128, 256], "float32"), "gcol2": ("sbuf", [128, 256], "float32"),
+    "blk": ("sbuf", [128, 128], "float32"), "mask": ("sbuf", [128, 128], "float32"),
+    "m2": ("sbuf", [128, 256], "bfloat16"), "mq": ("sbuf", [128, 128], "bfloat16"), "mx": ("sbuf", [128, 128], "bfloat16"),
+    "i2": ("sbuf", [128, 128], "float16"), "ni": ("sbuf", [128, 128], "float16"), "c8": ("sbuf", [128, 128], "float16"),
+    "iw": ("sbuf", [128, 17, 128], "bfloat16"), "bo": ("sbuf", [128, 128], "float16"), "tri": ("sbuf", [128, 128], "float16"),
+    "pos": ("sbuf", [128, 256], "float16"), "gs": ("sbuf", [128, 3, 8], "bfloat16"), "gs16": ("sbuf", [128, 8], "float16"),
+    "kc": ("sbuf", [128, 128], "float16"), "cl": ("sbuf", [128, 16], "uint16"), "dumt": ("sbuf", [128, 16], "float32"),
+    "nf": ("sbuf", [128, 2, 16], "float16"), "kk": ("sbuf", [128, 8], "float32"),
+    "r0c": ("sbuf", [128, 2, 128], "float16"), "rl": ("sbuf", [128, 8, 128], "float16"), "rn": ("sbuf", [128, 10, 128], "float16"),
+    "Xm": ("sbuf", [128, 256], "float16"), "XmT": ("sbuf", [128, 256], "float16"), "hexp": ("sbuf", [128, 256], "float32"),
+    "Sc": ("sbuf", [128, 256], "float32"), "Ed": ("sbuf", [128, 4, 256], "bfloat16"), "hw": ("sbuf", [128, 16], "float32"),
+    "ow": ("sbuf", [128, 16], "uint16"), "lw": ("sbuf", [128, 16], "uint16"), "t1": ("sbuf", [128, 2, 16], "float32"),
+    "Pq": ("psum", [128, 512], "float32"), "Pw": ("psum", [128, 32, 16], "float32"),
+}
+for _u in "01":
+    for _n in ("X", "F", "V", "X4", "W2"):
+        SCRATCH[_n + "h" + _u] = ("sbuf", [128, 128], "bfloat16")
+    for _n in ("q1", "q2", "q4", "q6", "HK", "RP", "S", "crow"):
+        SCRATCH[_n + "h" + _u] = ("sbuf", [128, 128], "float16")
+    SCRATCH["R1h" + _u] = ("sbuf", [128, 8, 16], "float16")
+    for _n in ("SA", "Y", "RB"):
+        SCRATCH[_n + "h" + _u] = ("sbuf", [128, 128], "float32")
+    for _n in ("La", "Lb"):
+        SCRATCH[_n + "h" + _u] = ("sbuf", [128, 128], "uint16")
+    for _n in ("Ga", "Gb", "da", "db", "yb"):
+        SCRATCH[_n + "h" + _u] = ("sbuf", [128, 2048], "bfloat16")
+    for _n in ("d2", "y2"):
+        SCRATCH[_n + "h" + _u] = ("sbuf", [128, 1024], "bfloat16")
+    SCRATCH["Eh" + _u] = ("sbuf", [128, 8, 8, 16], "bfloat16")
+    SCRATCH["rkh" + _u] = ("sbuf", [128, 4, 8], "float32")
+    SCRATCH["sih" + _u] = ("sbuf", [128, 4, 8], "int32")
+    SCRATCH["hmh" + _u] = ("sbuf", [128, 8], "int32")
+    SCRATCH["Pn" + _u] = ("psum", [128, 16, 32], "float32")
+    SCRATCH["Pd" + _u] = ("psum", [128, 512], "float32")
+    SCRATCH["Pt" + _u] = ("psum", [128, 512], "float32")
+
+DMAS = ["ldr", "ldx0", "ldx1", "ldc", "sty0", "sty1", "stc0", "stc1"]
+SEMAPHORES = ["qv", "qs", "qt", "qg", "sent"] + ["arr%d" % k for k in range(8)] + DMAS
+
+
+def rank_program(g, core, T, topo):
+    rank = T.rank_of(core)
+    if rank is None:
+        return
+    n_ranks = len(T.cores)
+    nxt = T.cores[(rank + 1) % n_ranks]
+    eng = {"v": g.vector, "s": g.scalar, "t": g.tensor, "g": g, "y": g.sync}
+    ops, lastw, readers, banks = [], {}, {}, {}
+
+    def add(q, fns, reads, writes, cost, sem=None, val=0, lat=0.0, deps=()):
+        k = len(ops)
+        need = set(deps)
+        for a in reads:
+            if a in lastw:
+                need.add(lastw[a])
+        for a in writes:
+            if a in lastw:
+                need.add(lastw[a])
+            need.update(readers.get(a, ()))
+        for a in set(a.split(":")[0] for a in list(reads) + list(writes) if a[0] == "P"):
+            acc = banks.setdefault(a, {})
+            need.update(i for qq, i in acc.items() if qq != q)
+            acc[q] = k
+        for a in reads:
+            readers.setdefault(a, []).append(k)
+        for a in writes:
+            lastw[a] = k
+            readers[a] = []
+        need.discard(k)
+        ops.append({"q": q, "f": fns, "need": need, "cost": cost, "sem": sem, "val": val, "lat": lat})
+        return k
+
+    def dur(n, c=1.0):
+        return CFG["vf"] + max(64.0, n * c) * 0.00083 * 1.1
+
+    def size(ap):
+        r = 1
+        for s in ap.shape[1:]:
+            r *= s
+        return r
+
+    def tt(out, a, b, op, c=None):
+        ps = a[0][0] == "P" or b[0][0] == "P"
+        n = size(out[1])
+        return add("v", [lambda: g.vector.tensor_tensor(out=out[1], in0=a[1], in1=b[1], op=op)], [a[0], b[0]], [out[0]], dur(n, c or (1 if ps else 2)))
+
+    def ts(out, a, s1, op0, s2=None, op1=None, c=1.0, extra=()):
+        n = size(out[1])
+        if op1 is None:
+            f = lambda: g.vector.tensor_scalar(out=out[1], in0=a[1], scalar1=s1, scalar2=None, op0=op0)
+        else:
+            f = lambda: g.vector.tensor_scalar(out=out[1], in0=a[1], scalar1=s1, scalar2=s2, op0=op0, op1=op1)
+        return add("v", [f], [a[0]] + list(extra), [out[0]], dur(n, c))
+
+    def cp(out, a, c=1.0, extra=()):
+        return add("v", [lambda: g.vector.tensor_copy(out=out[1], in_=a[1])], [a[0]] + list(extra), [out[0]], dur(size(out[1]), c))
+
+    def scan(out, a, b, op0, op1, c=1.0):
+        return add("v", [lambda: g.vector.tensor_tensor_scan(out=out[1], data0=a[1], data1=b[1], initial=0.0, op0=op0, op1=op1)],
+                   [a[0], b[0]], [out[0]], dur(size(out[1]), c))
+
+    def fill(key, ap, v):
+        return add("v", [lambda: g.vector.memset(ap, v)], [], [key], dur(size(ap)))
+
+    def act(out, a, func, bias=0.0, scale=1.0, c=1.0, extra=()):
+        return add("s", [lambda: g.scalar.activation(out=out[1], in_=a[1], func=func, bias=bias, scale=scale)],
+                   [a[0]] + list(extra), [out[0]], dur(size(out[1]), c))
+
+    def mm(items, reads, writes):
+        fns, cost = [], 0.04
+        for o, l, r, st, sp in items:
+            fns.append(lambda o=o, l=l, r=r, st=st, sp=sp: g.tensor.matmul(out=o, lhsT=l, rhs=r, start=st, stop=sp))
+            cost += max(64, size(r)) * 0.00083 * 0.6
+        return add("t", fns, reads, writes, cost)
+
+    def B(name, u=None):
+        nm = name if u is None else "%sh%d" % (name, u)
+        return (nm, T[nm][:])
+
+    add("y", [lambda: g.sync.dma_start(T.ri[:], T.r0[:])], [], ["ri"], 0.1, "ldr", 16, 2.5)
+    add("s", [lambda: g.scalar.dma_start(T.xw[0:64, :], T.x[0:64, :])], [], ["xw"], 0.1, "ldx0", 16, 6.0)
+    add("y", [lambda: g.sync.dma_start(T.xw[64:128, :], T.x[64:128, :])], [], ["xw_"], 0.1, "ldx1", 16, 6.5)
+    add("y", [lambda: g.sync.dma_start(T.ci[:], T.c0[:])], [], ["ci"], 0.1, "ldc", 16, 10.0)
+
+    add("g", [lambda: g.iota(T.pint[:, 0:1], [[0, 1]], 0, 1)], [], ["pint"], 0.2)
+    add("g", [lambda: g.iota(T.icol2[:], [[0, 16], [1, 16]], 0, 0, allow_small_or_imprecise_dtypes=True)], [], ["icol2"], 0.6)
+    add("g", [lambda: g.iota(T.gcol2[:], [[1, 16], [0, 16]], 0, 0, allow_small_or_imprecise_dtypes=True)], [], ["gcol2"], 0.6)
+    for u in (0, 1):
+        cp(B("La", u), ("ri", T.ri[:, 128 * u:128 * u + 128]))
+        ts(B("crow", u), ("ri", T.ri[:, 128 * u:128 * u + 128]), -OFF, OP.add)
+    ts(("pi2a", T.pint[:, 1:2]), ("pint", T.pint[:, 0:1]), 15, OP.bitwise_and)
+    ts(("pi2b", T.pint[:, 2:3]), ("pint", T.pint[:, 0:1]), 4, OP.arith_shift_right)
+    cp(("pmod", T.pf[:, 0:1]), ("pi2a", T.pint[:, 1:2]))
+    cp(("pdiv", T.pf[:, 1:2]), ("pi2b", T.pint[:, 2:3]))
+    pmod, pdiv = T.pf[:, 0:1], T.pf[:, 1:2]
+    ic, gc_ = ("icol2", T.icol2[:, 0:128]), ("gcol2", T.gcol2[:, 0:128])
+    heads = ("blk", T.blk[:, 0:128:16])
+    ts(B("mask"), ic, pmod, OP.is_equal, extra=["pmod"])
+    ts(B("blk"), gc_, pdiv, OP.is_equal, extra=["pdiv"])
+    tt(B("i2"), B("mask"), B("blk"), OP.mult)
+    ts(B("ni"), B("i2"), -1.0, OP.mult)
+    ts(B("c8"), ic, 0.0, OP.mult, NO, OP.add)
+    ts(B("kc"), ic, 0.0, OP.mult, -1.0 / OFF, OP.add)
+    cp(("gs0", T.gs[:, 0, :]), heads)
+    ts(("gs1", T.gs[:, 1, :]), heads, 2.0, OP.mult)
+    ts(("gs2", T.gs[:, 2, :]), heads, -1.0, OP.mult)
+    cp(B("gs16"), heads)
+    ts(B("m2"), B("icol2"), 0.0, OP.is_gt)
+    ts(B("mq"), ic, 0.0, OP.is_gt, 0.25, OP.mult)
+    cp(B("mx"), ("m2", T.m2[:, 0:128]))
+    fill("mx", T.mx[:, 15:128:16], 0.0)
+    cp(B("cl"), ("gcol2", T.gcol2[:, 0:256:16]))
+    cp(B("bo"), B("blk"))
+    ts(B("tri"), ic, pmod, OP.is_gt, extra=["pmod"])
+    tt(B("tri"), B("tri"), B("blk"), OP.mult)
+    ts(B("pos"), B("icol2"), pmod, OP.is_ge, OFF, OP.mult, extra=["pmod"])
+    ts(B("dumt"), ("gcol2", T.gcol2[:, 0:256:16]), 16.0, OP.mult, pmod, OP.add, extra=["pmod"])
+    ts(B("dumt"), B("dumt"), OFF, OP.add)
+    cp(("iw0", T.iw[:, 0, :]), B("i2"))
+    for d in range(1, 16):
+        act(("iw%d" % d, T.iw[:, d, :]), ("iw0", T.iw[:, 0, :]), ID, 0.0, float(4 ** d))
+    act(("iw16", T.iw[:, 16, :]), ("iw0", T.iw[:, 0, :]), ID, 0.0, -BIG)
+    for u in (0, 1):
+        P = T["Pd%d" % u]
+        fill("Pd%d:D1" % u, P[:, 0:128], 0.0)
+        fill("Pd%d:D2" % u, P[:, 128:256], 10000.0)
+        ts(B("q6", u), ic, 0.0, OP.mult, NO, OP.add)
+    fill("Pw:0", T.Pw[:, 0:8, :], 0.0)
+    fill("Pw:1", T.Pw[:, 8:16, :], 0.0)
+    fill("cw", T.cw[:, 2048:CW], 0.0)
+    for k in range(2):
+        cp(("cw", T.cw[:, 1024 * k:1024 * k + 1024]), ("ci", T.ci[:, 1024 * k:1024 * k + 1024]))
+    for u in (0, 1):
+        Pt = T["Pt%d" % u]
+        mm([(Pt[:, 0:128], T["crowh%d" % u][:], T.i2[:], True, True)], ["crowh%d" % u, "i2"], ["Pt%d:A" % u])
+        cp(("r0c%d" % u, T.r0c[:, u, :]), ("Pt%d:A" % u, Pt[:, 0:128]))
+
+    def gather(u, st):
+        L, G = T["L%sh%d" % (st, u)], T["G%sh%d" % (st, u)]
+        kl, win = "L%sh%d" % (st, u), T.xw[:, 0:4096]
+        nch, ndve = CFG["ch_" + st], CFG["gv_" + st]
+        for ch in range(nch):
+            a, b = 128 // nch * ch, 128 // nch * (ch + 1)
+            key = "G%sh%d.%d" % (st, u, ch)
+            parts = []
+            if ch == nch - 1 and ndve:
+                parts = [("v", b - ndve, b)]
+                b -= ndve
+            parts.append(("s", a, b))
+            for q, a, b in parts:
+                o, i = G[:, 16 * a:16 * b], win.indirect(L[:, a:b])
+                if q == "s":
+                    act((key + q, o), ("xw", i), ID, 16.0, c=CFG["gam"], extra=["xw_", kl])
+                else:
+                    ts((key + q, o), ("xw", i), 16.0, OP.add, c=CFG["gam"], extra=["xw_", kl])
+
+    def dist(u, st, step):
+        G = T["G%sh%d" % (st, u)]
+        dn = "d2" if step == 2 else "d" + st
+        absact = CFG["abs_2" if step == 2 else "abs_" + st]
+        d = T["%sh%d" % (dn, u)]
+        y = d if absact else T["%sh%d" % ("y2" if step == 2 else "y" + st, u)]
+        nch = CFG["ch_" + st]
+        w = 2048 // nch
+        n = w // step
+        for ch in range(nch):
+            a, b = w * ch, w * ch + w
+            key = "G%sh%d.%d" % (st, u, ch)
+            kd, ky = "%sh%d.%d" % (dn, u, ch), "%sh%d.%d%s" % (dn, u, ch, "" if absact else "y")
+            o = d[:, n * ch:n * ch + n - 1]
+            add("v", [lambda o=o, a=a, b=b: g.vector.tensor_tensor_scan(out=o, data0=G[:, a:b - step:step], data1=G[:, a + step:b:step], initial=0.0, op0=OP.max, op1=OP.subtract)],
+                [key + "s", key + "v"], [kd], dur(n, 0.5))
+            yo = y[:, n * ch:n * ch + n - 1]
+            if absact:
+                act((ky, yo), (kd, o), ABS)
+            else:
+                ts((ky, yo), (kd, o), 0.0, OP.max, c=0.5)
+
+    def sums(u, st, step):
+        dn = "d2" if step == 2 else "d" + st
+        absact = CFG["abs_2" if step == 2 else "abs_" + st]
+        d = T["%sh%d" % (dn, u)]
+        P = T["Pd%d" % u]
+        items, wr = [], ["Pd%d:%s" % (u, "D1" if step == 1 else "D2")]
+        per = 16 // step
+        for p in range(7 if step == 2 else 15 if st == "a" else 14):
+            if step == 2:
+                o = P[:, 129 + 2 * p:256:16]
+            elif p < 14:
+                o = P[:, p + 1:128:16]
+            else:
+                o = P[:, 128:256:16]
+                wr.append("Pd%d:D2" % u)
+            if absact:
+                items.append((o, d[:, p:128 * per:per], T.gs[:, 0, :], True, True))
+            else:
+                y = T["%sh%d" % ("y2" if step == 2 else "y" + st, u)]
+                items.append((o, y[:, p:128 * per:per], T.gs[:, 1, :], True, False))
+                items.append((o, d[:, p:128 * per:per], T.gs[:, 2, :], False, True))
+        chs = range(CFG["ch_" + st])
+        rd = ["gs0", "gs1", "gs2"] + ["%sh%d.%d" % (dn, u, ch) for ch in chs] + ([] if absact else ["%sh%d.%dy" % (dn, u, ch) for ch in chs])
+        mm(items, rd, wr)
+
+    def hold(u, reg, out, q, rk, r):
+        P = T["Pd%d" % u]
+        z = {"C": 256, "RB": 384}[reg]
+        kp = "Pd%d:%s" % (u, reg)
+        o = P[:, z:z + 128]
+        mm([(o, T.i2[:], r, True, False), (o, T.i2[:], T.c8[:], False, False), (o, T.ni[:], q[1], False, True)], [rk, q[0], "i2", "c8", "ni"], [kp])
+        scan(out, q, (kp, o), OP.add, OP.max)
+        return kp, o
+
+    def stage_a(t, u):
+        Pn, Pd, Pt = T["Pn%d" % u], T["Pd%d" % u], T["Pt%d" % u]
+        kn, kt, kX = "Pn%d:R" % u, "Pt%d:A" % u, "Xh%d" % u
+        if t == 0:
+            slot, r = "r0c%d" % u, T.r0c[:, u, :]
+        else:
+            slot, r = "rl%d" % (2 * (t - 1) + u), T.rl[:, 2 * (t - 1) + u, :]
+            mm([(Pt[:, 0:128], r, T.i2[:], True, True)], [slot, "i2"], [kt])
+            ts(B("La", u), (kt, Pt[:, 0:128]), OFF, OP.add)
+        gather(u, "a")
+        dist(u, "a", 1)
+        sums(u, "a", 1)
+        X = T["Xh%d" % u]
+        scan(B("X", u), B("mx"), ("Pd%d:D1" % u, Pd[:, 0:128]), OP.mult, OP.max)
+        ts(B("q1", u), B("X", u), TH, OP.is_le, NO, OP.mult, c=0.5)
+        kp, rb = hold(u, "RB", B("HK", u), B("q1", u), slot, r)
+        sm, si = T["rkh%d" % u], T["sih%d" % u]
+        ks, kr = "sih%d." % u, "rkh%d." % u
+        HK = T["HKh%d" % u]
+        ts((kr + "rk", sm[:, 0, :]), ("HKh%d" % u, HK[:, 14:128:16]), OFF, OP.add)
+        ts((kr + "r15", sm[:, 1, :]), (kp, Pd[:, 399:512:16]), OFF, OP.add)
+        tt((ks + "prod", si[:, 0, :]), (kr + "rk", sm[:, 0, :]), (kr + "r15", sm[:, 1, :]), OP.mult)
+        rk = (kr + "rk", sm[:, 0, :])
+        if t > 0:
+            rk = (kr + "rkK", sm[:, 2, :])
+            ts(rk, ("HKh%d" % u, HK[:, 14:128:16]), OFF + 2048.0, OP.add, T.kk[:, t - 1:t], OP.add, extra=["kk%d" % (t - 1)])
+        ts((ks + "sh", si[:, 1, :]), (ks + "prod", si[:, 0, :]), 6, OP.arith_shift_right)
+        tt((ks + "s", si[:, 2, :]), (ks + "sh", si[:, 1, :]), rk, OP.add)
+        ts((ks + "h", si[:, 3, :]), (ks + "s", si[:, 2, :]), 2047, OP.bitwise_and)
+        act(B("RB", u), (kp, rb), ID)
+        tt((kr + "xf", sm[:, 3, :]), (kX, X[:, 14:128:16]), ("Pd%d:D2" % u, Pd[:, 128:256:16]), OP.max)
+        nf = ("nf%d.%d" % (t % 2, u), T.nf[:, t % 2, 8 * u:8 * u + 8])
+        ts(nf, (kr + "xf", sm[:, 3, :]), TH, OP.is_le, OFF, OP.mult)
+        tt(B("hm", u), (ks + "h", si[:, 3, :]), nf, OP.max)
+        Xm = T.Xm[:, 128 * u:128 * u + 128]
+        add("v", [lambda: g.vector.tensor_tensor(out=Xm, in0=T["hmh%d" % u][:, 0:8].indirect(T.cl[:, 0:8]), in1=T.mask[:], op=OP.mult)],
+            ["hmh%d" % u, "cl", "mask"], ["Xm%d" % u], dur(128, CFG["gam"]))
+        mm([(Pt[:, 0:8], Xm, T.gs16[:], True, True)], ["Xm%d" % u, "gs16"], [kt])
+        ow = ("ow%d" % u, T.ow[:, 8 * u:8 * u + 8])
+        cp(ow, (kt, Pt[:, 0:8]))
+        ts(B("crow", u), ("cw", T.cw[:, 0:CW].indirect(ow[1])), -OFF, OP.add, c=CFG["gam"], extra=[ow[0]])
+        kc, C = "Pd%d:C" % u, Pd[:, 256:384]
+        mm([(C, T["crowh%d" % u][:], T.i2[:], True, False), (C, T.i2[:], T["q1h%d" % u][:], False, True)], ["crowh%d" % u, "q1h%d" % u, "i2"], [kc])
+        tt(B("R1", u), B("RB", u), (kc, C), OP.max)
+        R1, E = T["R1h%d" % u], T["Eh%d" % u]
+        mm([(Pn[:, 0:8, 0:16], T.i2[:], R1[:], True, True), (Pn[:, 0:8, 16:24], T.i2[:], R1[:, :, 0:8], True, True)], ["R1h%d" % u, "i2"], [kn])
+        kw, W = "Pw:%d" % u, T.Pw[:, 8 * u:8 * u + 8, :]
+        for d in range(1, 9):
+            n = 16 if d < 8 else 8
+            ke, e = "Eh%d.%d" % (u, d), 16 - d
+            tt((ke, E[:, d - 1, :, 0:n]), ("R1h%d" % u, R1[:, :, 0:n]), (kn, Pn[:, 0:8, d:d + n]), OP.is_equal)
+            its = [(T.Pw[:, 8 * u:8 * u + 8, 1:e + 1], T.iw[:, d, :], E[:, d - 1, :, 0:e], d == 1, d == 8)]
+            if d < 8:
+                its.append((T.Pw[:, 8 * u:8 * u + 8, 1:d + 1], T.iw[:, e, :], E[:, d - 1, :, e:16], False, False))
+            mm(its, [ke, "iw%d" % d, "iw%d" % e], [kw])
+        cp(B("W2", u), (kw, W))
+        scan(B("F", u), ("m2", T.m2[:, 0:128]), B("W2", u), OP.mult, OP.max, 0.5)
+        mm([(C, T.iw[:, 0, :], T["W2h%d" % u][:], True, False), (Pd[:, 257:384], T.iw[:, 16, :], T["Fh%d" % u][:, 0:127], False, True)],
+           ["W2h%d" % u, "Fh%d" % u, "iw0", "iw16"], [kc])
+        scan(B("V", u), B("mq"), (kc, C), OP.mult, OP.max)
+        ts(B("q2", u), B("V", u), 4.0, OP.is_lt, NO, OP.mult, c=0.5)
+        hold(u, "RB", B("RP", u), B("q2", u), "R1h%d" % u, R1[:])
+        mm([(Pt[:, 0:128], T["RPh%d" % u][:], T.i2[:], True, True)], ["RPh%d" % u, "i2"], [kt])
+        ts(B("Lb", u), (kt, Pt[:, 0:128]), OFF, OP.add)
+
+    def stage_b(t, u):
+        Pd, Pt = T["Pd%d" % u], T["Pt%d" % u]
+        kt = "Pt%d:A" % u
+        RP = T["RPh%d" % u][:]
+        gather(u, "b")
+        dist(u, "b", 2)
+        dist(u, "b", 1)
+        sums(u, "b", 2)
+        ts(("q6h%d" % u, T["q6h%d" % u][:, 1:128:2]), ("Pd%d:D2" % u, Pd[:, 129:256:2]), TH, OP.is_gt, NO, OP.mult)
+        k = 2 * t + u
+        slot, rn = "rn%d" % k, T.rn[:, k, :]
+        hold(u, "RB", (slot, rn), B("q6", u), "RPh%d" % u, RP)
+        if t < ROUNDS - 1:
+            rid, pid, _s = topo.addr(nxt)
+            m = 0
+            for e in topo.engines(core, nxt)[:NENG]:
+                m |= 1 << e
+            sd = add("g", [lambda: g.remote_dma(out_ap=T.rl[:, k, :], in_ap=rn, remote_sem=T.sem["arr%d" % k], local_sem=T.sem.sent, pid=pid, routing_id=rid, dma_engine_mask=m)],
+                     [slot], [], 0.3, "none", 0, 1.7)
+            add(None, [], [], ["rl%d" % k], 0.0, "arr%d" % k, NENG, 0.0, deps=[sd])
+        sums(u, "b", 1)
+        scan(B("X4", u), B("mx"), ("Pd%d:D1" % u, Pd[:, 0:128]), OP.mult, OP.max)
+        ts(B("q4", u), B("X4", u), TH, OP.is_le, NO, OP.mult, c=0.5)
+        hold(u, "C", B("S", u), B("q4", u), "RPh%d" % u, RP)
+        mm([(Pt[:, 0:128], T["Sh%d" % u][:], T.i2[:], True, True)], ["Sh%d" % u, "i2"], [kt])
+        act(B("SA", u), (kt, Pt[:, 0:128]), ID, OFF)
+        if t == ROUNDS - 1:
+            mm([(Pt[:, 128:256], rn, T.i2[:], True, True)], [slot, "i2"], ["Pt%d:Y" % u])
+            act(B("Y", u), ("Pt%d:Y" % u, Pt[:, 128:256]), ID, OFF)
+            add("y", [lambda: g.sync.dma_start(T.yr[:, 128 * u:128 * u + 128], T["Yh%d" % u][:])], ["Yh%d" % u], [], 0.1, "sty%d" % u, 16, 2.0)
+
+    def count(t):
+        f = T.nf[:, t % 2, :]
+        mm([(T.Pt1[:, 256:272], T.kc[:], f, True, True)], ["nf%d.0" % (t % 2), "nf%d.1" % (t % 2), "kc"], ["Pt1:K"])
+        add("v", [lambda: g.vector.tensor_reduce(out=T.kk[:, t:t + 1], in_=T.Pt1[:, 256:272], axis=AxisListType.X, op=OP.add)], ["Pt1:K"], ["kk%d" % t], dur(16))
+
+    def winners():
+        q = T.Pq
+        mm([(q[:, 128 * u:128 * u + 128], T.Xm[:, 128 * u:128 * u + 128], T.i2[:], True, True) for u in (0, 1)], ["Xm0", "Xm1", "i2"], ["Pq:L"])
+        cp(B("XmT"), ("Pq:L", q[:, 0:256]))
+        cp(B("hw"), ("ow0", T.ow[:]), extra=["ow1"])
+        act(B("hexp"), ("hw", T.hw[:, 0:16].indirect(T.cl[:, 0:16])), ID, c=CFG["gam"], extra=["cl"])
+        mm([(q[:, 0:256], T.bo[:], T.XmT[:], True, True)], ["XmT", "bo"], ["Pq:L"])
+        mm([(q[:, 256:512], T.tri[:], T.XmT[:], True, False), (q[:, 256:512], T.i2[:], T.pos[:], False, True)], ["XmT", "tri", "i2", "pos"], ["Pq:R"])
+        for k in range(4):
+            w = 256 - 16 * k
+            a = ("Pq:R", q[:, 256:512]) if k == 0 else ("Pq:L", q[:, 0:w])
+            tt(("Ed%d" % k, T.Ed[:, k, 0:w]), ("hexp", T.hexp[:, 16 * k:256]), a, OP.is_equal)
+        mm([(q[:, 16 * k:256], T.iw[:, 6, :], T.Ed[:, k, 0:256 - 16 * k], k == 0, k == 3) for k in range(4)],
+           ["Ed%d" % k for k in range(4)] + ["iw6"], ["Pq:L"])
+        scan(B("Sc"), B("m2"), ("Pq:L", q[:, 0:256]), OP.mult, OP.max)
+        tt(("t1a", T.t1[:, 0, :]), ("Sc", T.Sc[:, 15:256:16]), B("dumt"), OP.min)
+        tt(("t1b", T.t1[:, 1, :]), ("t1a", T.t1[:, 0, :]), B("hw"), OP.max)
+        cp(B("lw"), ("t1b", T.t1[:, 1, :]))
+
+    def scatter(u):
+        for k in (1, 0):
+            o = T.cw[:, 0:CW].indirect(T.lw[:, 8 * u + 4 * k:8 * u + 4 * k + 4])
+            add("v", [lambda o=o, k=k: g.vector.tensor_copy(out=o, in_=T["SAh%d" % u][:, 64 * k:64 * k + 64])], ["SAh%d" % u, "lw"], ["cw"], dur(64, 3.5))
+
+    for t in range(ROUNDS):
+        stage_a(t, 0)
+        stage_a(t, 1)
+        if t < ROUNDS - 1:
+            count(t)
+        winners()
+        stage_b(t, 0)
+        stage_b(t, 1)
+        scatter(1)
+        scatter(0)
+    add("s", [lambda: g.scalar.dma_start(T.yc[0:64, :], T.cw[0:64, 0:2048])], ["cw"], [], 0.1, "stc0", 16, 5.0)
+    add("y", [lambda: g.sync.dma_start(T.yc[64:128, :], T.cw[64:128, 0:2048])], ["cw"], [], 0.1, "stc1", 16, 5.0)
+
+    n = len(ops)
+    users = [[] for _ in range(n)]
+    for k, o in enumerate(ops):
+        for d in o["need"]:
+            users[d].append(k)
+    way = [0.0] * n
+    for k in range(n - 1, -1, -1):
+        o = ops[k]
+        way[k] = o["cost"] + o["lat"] + CFG["wake"] + max([way[j] for j in users[k]] or [0.0])
+    left = [len(o["need"]) for o in ops]
+    at = [0.0] * n
+    free = {q: 0.0 for q in ("v", "s", "t", "g", "y", None)}
+    pool = [k for k in range(n) if left[k] == 0]
+    order = []
+    while pool:
+        best, bs = None, None
+        for k in pool:
+            o = ops[k]
+            st = max(free[o["q"]] if o["q"] else 0.0, at[k])
+            key = (st, -way[k])
+            if bs is None or key < bs:
+                best, bs = k, key
+        pool.remove(best)
+        o = ops[best]
+        st = bs[0]
+        if o["q"]:
+            free[o["q"]] = st + o["cost"]
+        done = st + o["cost"] + o["lat"]
+        order.append(best)
+        for j in users[best]:
+            lag = 0.0 if ops[j]["q"] == o["q"] == "t" else CFG["wake"]
+            at[j] = max(at[j], done + lag)
+            left[j] -= 1
+            if left[j] == 0:
+                pool.append(j)
+
+    total = {"qv": 0, "qs": 0, "qt": 0, "qg": 0}
+    known = {q: {} for q in eng}
+    for k in order:
+        o = ops[k]
+        q = o["q"]
+        if q is None:
+            continue
+        want = {}
+        for d in o["need"]:
+            p = ops[d]
+            if p["sem"] == "none" or (p["q"] == q and q == "t"):
+                continue
+            want[p["sem"]] = max(want.get(p["sem"], 0), p["val"])
+        for s in sorted(want):
+            if known[q].get(s, 0) < want[s]:
+                known[q][s] = want[s]
+                eng[q].wait_ge(T.sem[s], want[s])
+        fresh = o["sem"] is None
+        for f in o["f"]:
+            ins = f()
+            if fresh:
+                o["sem"] = "q" + q
+                total["q" + q] += 1
+                o["val"] = total["q" + q]
+                ins.then_inc(T.sem["q" + q], 1)
+            elif o["sem"] != "none":
+                ins.then_inc(T.sem[o["sem"]], 16)
+    for s in sorted(total):
+        g.wait_ge(T.sem[s], total[s])
+    for s in DMAS:
+        g.wait_ge(T.sem[s], 16)
+    g.wait_ge(T.sem.sent, 2 * (ROUNDS - 1) * NENG)

@@ -10,7 +10,11 @@ NO = -8192.0
 CW = 2048 + 256
 NENG = 8
 BIG = float(2 ** 40)
-CFG = {"abs_a": True, "abs_b": False, "abs_2": True, "gv_a": 0, "gv_b": 0, "ch_a": 1, "ch_b": 1, "vf": 0.04, "wake": 0.08, "gam": 1.5}
+CFG = {"abs_a": True, "abs_b": False, "abs_2": True,
+       "gv_a": 16, "gv_b": 16, "gv0": (32, 64),
+       "ch_a": 2, "ch_b": 2,
+       "vf": 0.04, "wake": 0.1, "gam": 1.5,
+       "b0": 3.0, "bb": -4.0, "bs": -2.0, "ww": 0.005}
 
 SCRATCH = {
     "xw": ("sbuf", [128, 4096], "bfloat16"), "cw": ("sbuf", [128, CW], "float32"), "ci": ("sbuf", [128, 2048], "int32"),
@@ -63,6 +67,7 @@ def rank_program(g, core, T, topo):
     nxt = T.cores[(rank + 1) % n_ranks]
     eng = {"v": g.vector, "s": g.scalar, "t": g.tensor, "g": g, "y": g.sync}
     ops, lastw, readers, banks = [], {}, {}, {}
+    cur = [0.0]
 
     def add(q, fns, reads, writes, cost, sem=None, val=0, lat=0.0, deps=()):
         k = len(ops)
@@ -75,16 +80,16 @@ def rank_program(g, core, T, topo):
                 need.add(lastw[a])
             need.update(readers.get(a, ()))
         for a in set(a.split(":")[0] for a in list(reads) + list(writes) if a[0] == "P"):
-            acc = banks.setdefault(a, {})
-            need.update(i for qq, i in acc.items() if qq != q)
-            acc[q] = k
+            acc = banks.setdefault(a, [])
+            need.update(i for qq, i in acc[-48:] if qq != q)
+            acc.append((q, k))
         for a in reads:
             readers.setdefault(a, []).append(k)
         for a in writes:
             lastw[a] = k
             readers[a] = []
         need.discard(k)
-        ops.append({"q": q, "f": fns, "need": need, "cost": cost, "sem": sem, "val": val, "lat": lat})
+        ops.append({"q": q, "f": fns, "need": need, "cost": cost, "sem": sem, "val": val, "lat": lat, "b": cur[0]})
         return k
 
     def dur(n, c=1.0):
@@ -137,7 +142,7 @@ def rank_program(g, core, T, topo):
     add("y", [lambda: g.sync.dma_start(T.ri[:], T.r0[:])], [], ["ri"], 0.1, "ldr", 16, 2.5)
     add("s", [lambda: g.scalar.dma_start(T.xw[0:64, :], T.x[0:64, :])], [], ["xw"], 0.1, "ldx0", 16, 6.0)
     add("y", [lambda: g.sync.dma_start(T.xw[64:128, :], T.x[64:128, :])], [], ["xw_"], 0.1, "ldx1", 16, 6.5)
-    add("y", [lambda: g.sync.dma_start(T.ci[:], T.c0[:])], [], ["ci"], 0.1, "ldc", 16, 10.0)
+    add("y", [lambda: g.sync.dma_start(T.ci[:], T.c0[:])], [], ["ci"], 0.1, "ldc", 16, 5.5, deps=(1, 2))
 
     add("g", [lambda: g.iota(T.pint[:, 0:1], [[0, 1]], 0, 1)], [], ["pint"], 0.2)
     add("g", [lambda: g.iota(T.icol2[:], [[0, 16], [1, 16]], 0, 0, allow_small_or_imprecise_dtypes=True)], [], ["icol2"], 0.6)
@@ -157,7 +162,7 @@ def rank_program(g, core, T, topo):
     tt(B("i2"), B("mask"), B("blk"), OP.mult)
     ts(B("ni"), B("i2"), -1.0, OP.mult)
     ts(B("c8"), ic, 0.0, OP.mult, NO, OP.add)
-    ts(B("kc"), ic, 0.0, OP.mult, -1.0 / OFF, OP.add)
+    ts(B("kc"), ic, 0.0, OP.mult, -64.0 / OFF, OP.add)
     cp(("gs0", T.gs[:, 0, :]), heads)
     ts(("gs1", T.gs[:, 1, :]), heads, 2.0, OP.mult)
     ts(("gs2", T.gs[:, 2, :]), heads, -1.0, OP.mult)
@@ -192,10 +197,12 @@ def rank_program(g, core, T, topo):
         mm([(Pt[:, 0:128], T["crowh%d" % u][:], T.i2[:], True, True)], ["crowh%d" % u, "i2"], ["Pt%d:A" % u])
         cp(("r0c%d" % u, T.r0c[:, u, :]), ("Pt%d:A" % u, Pt[:, 0:128]))
 
-    def gather(u, st):
+    def gather(u, st, t):
         L, G = T["L%sh%d" % (st, u)], T["G%sh%d" % (st, u)]
         kl, win = "L%sh%d" % (st, u), T.xw[:, 0:4096]
         nch, ndve = CFG["ch_" + st], CFG["gv_" + st]
+        if t == 0 and st == "a":
+            ndve = CFG["gv0"][u]
         for ch in range(nch):
             a, b = 128 // nch * ch, 128 // nch * (ch + 1)
             key = "G%sh%d.%d" % (st, u, ch)
@@ -203,7 +210,8 @@ def rank_program(g, core, T, topo):
             if ch == nch - 1 and ndve:
                 parts = [("v", b - ndve, b)]
                 b -= ndve
-            parts.append(("s", a, b))
+            if b > a:
+                parts.append(("s", a, b))
             for q, a, b in parts:
                 o, i = G[:, 16 * a:16 * b], win.indirect(L[:, a:b])
                 if q == "s":
@@ -276,7 +284,7 @@ def rank_program(g, core, T, topo):
             slot, r = "rl%d" % (2 * (t - 1) + u), T.rl[:, 2 * (t - 1) + u, :]
             mm([(Pt[:, 0:128], r, T.i2[:], True, True)], [slot, "i2"], [kt])
             ts(B("La", u), (kt, Pt[:, 0:128]), OFF, OP.add)
-        gather(u, "a")
+        gather(u, "a", t)
         dist(u, "a", 1)
         sums(u, "a", 1)
         X = T["Xh%d" % u]
@@ -286,16 +294,15 @@ def rank_program(g, core, T, topo):
         sm, si = T["rkh%d" % u], T["sih%d" % u]
         ks, kr = "sih%d." % u, "rkh%d." % u
         HK = T["HKh%d" % u]
-        ts((kr + "rk", sm[:, 0, :]), ("HKh%d" % u, HK[:, 14:128:16]), OFF, OP.add)
-        ts((kr + "r15", sm[:, 1, :]), (kp, Pd[:, 399:512:16]), OFF, OP.add)
-        tt((ks + "prod", si[:, 0, :]), (kr + "rk", sm[:, 0, :]), (kr + "r15", sm[:, 1, :]), OP.mult)
-        rk = (kr + "rk", sm[:, 0, :])
+        ts((ks + "q", si[:, 0, :]), (kp, Pd[:, 399:512:16]), OFF + 64.0, OP.add)
+        ts((ks + "m", si[:, 1, :]), (ks + "q", si[:, 0, :]), 63, OP.bitwise_and)
         if t > 0:
-            rk = (kr + "rkK", sm[:, 2, :])
-            ts(rk, ("HKh%d" % u, HK[:, 14:128:16]), OFF + 2048.0, OP.add, T.kk[:, t - 1:t], OP.add, extra=["kk%d" % (t - 1)])
-        ts((ks + "sh", si[:, 1, :]), (ks + "prod", si[:, 0, :]), 6, OP.arith_shift_right)
-        tt((ks + "s", si[:, 2, :]), (ks + "sh", si[:, 1, :]), rk, OP.add)
-        ts((ks + "h", si[:, 3, :]), (ks + "s", si[:, 2, :]), 2047, OP.bitwise_and)
+            ts((kr + "b", sm[:, 2, :]), (ks + "m", si[:, 1, :]), 2048.0, OP.mult, T.kk[:, t - 1:t], OP.add, extra=["kk%d" % (t - 1)])
+        else:
+            ts((kr + "b", sm[:, 2, :]), (ks + "m", si[:, 1, :]), 2048.0, OP.mult)
+        tt((kr + "p", sm[:, 0, :]), ("HKh%d" % u, HK[:, 14:128:16]), (ks + "q", si[:, 0, :]), OP.mult)
+        tt((ks + "s", si[:, 2, :]), (kr + "p", sm[:, 0, :]), (kr + "b", sm[:, 2, :]), OP.add)
+        ts((ks + "h", si[:, 3, :]), (ks + "s", si[:, 2, :]), 6, OP.arith_shift_right, 2047, OP.bitwise_and)
         act(B("RB", u), (kp, rb), ID)
         tt((kr + "xf", sm[:, 3, :]), (kX, X[:, 14:128:16]), ("Pd%d:D2" % u, Pd[:, 128:256:16]), OP.max)
         nf = ("nf%d.%d" % (t % 2, u), T.nf[:, t % 2, 8 * u:8 * u + 8])
@@ -336,7 +343,7 @@ def rank_program(g, core, T, topo):
         Pd, Pt = T["Pd%d" % u], T["Pt%d" % u]
         kt = "Pt%d:A" % u
         RP = T["RPh%d" % u][:]
-        gather(u, "b")
+        gather(u, "b", t)
         dist(u, "b", 2)
         dist(u, "b", 1)
         sums(u, "b", 2)
@@ -393,13 +400,18 @@ def rank_program(g, core, T, topo):
             add("v", [lambda o=o, k=k: g.vector.tensor_copy(out=o, in_=T["SAh%d" % u][:, 64 * k:64 * k + 64])], ["SAh%d" % u, "lw"], ["cw"], dur(64, 3.5))
 
     for t in range(ROUNDS):
+        cur[0] = CFG["b0"]
         stage_a(t, 0)
+        cur[0] = 0.0
         stage_a(t, 1)
         if t < ROUNDS - 1:
             count(t)
         winners()
+        cur[0] = CFG["b0"] + CFG["bb"]
         stage_b(t, 0)
+        cur[0] = CFG["bb"]
         stage_b(t, 1)
+        cur[0] = CFG["bs"]
         scatter(1)
         scatter(0)
     add("s", [lambda: g.scalar.dma_start(T.yc[0:64, :], T.cw[0:64, 0:2048])], ["cw"], [], 0.1, "stc0", 16, 5.0)
@@ -414,22 +426,23 @@ def rank_program(g, core, T, topo):
     for k in range(n - 1, -1, -1):
         o = ops[k]
         way[k] = o["cost"] + o["lat"] + CFG["wake"] + max([way[j] for j in users[k]] or [0.0])
+    way = [w + o["b"] for w, o in zip(way, ops)]
     left = [len(o["need"]) for o in ops]
     at = [0.0] * n
     free = {q: 0.0 for q in ("v", "s", "t", "g", "y", None)}
     pool = [k for k in range(n) if left[k] == 0]
     order = []
     while pool:
-        best, bs = None, None
+        best, bs, bst = None, None, 0.0
         for k in pool:
             o = ops[k]
             st = max(free[o["q"]] if o["q"] else 0.0, at[k])
-            key = (st, -way[k])
+            key = (st - CFG["ww"] * way[k], -way[k])
             if bs is None or key < bs:
-                best, bs = k, key
+                best, bs, bst = k, key, st
         pool.remove(best)
         o = ops[best]
-        st = bs[0]
+        st = bst
         if o["q"]:
             free[o["q"]] = st + o["cost"]
         done = st + o["cost"] + o["lat"]
@@ -440,6 +453,7 @@ def rank_program(g, core, T, topo):
             left[j] -= 1
             if left[j] == 0:
                 pool.append(j)
+    CFG["ms"] = max(free.values())
 
     total = {"qv": 0, "qs": 0, "qt": 0, "qg": 0}
     known = {q: {} for q in eng}

from concourse.mybir import AluOpType, AxisListType, ActivationFunctionType

OP = AluOpType
ID = ActivationFunctionType.Identity
ABS = ActivationFunctionType.Abs
ROUNDS = 5
TH = 36.0
OFF = 2048.0
NO = -8192.0
CW = 2048 + 256
NENG = 8
BIG = float(2 ** 40)
CFG = {"abs_a": True, "abs_b": False, "abs_2": True,
       "gv_a": 16, "gv_b": 16, "gv0": (32, 64),
       "ch_a": 2, "ch_b": 2,
       "vf": 0.04, "wake": 0.1, "gam": 1.5,
       "b0": 3.0, "bb": -4.0, "bs": -2.0, "ww": 0.005}

SCRATCH = {
    "xw": ("sbuf", [128, 4096], "bfloat16"), "cw": ("sbuf", [128, CW], "float32"), "ci": ("sbuf", [128, 2048], "int32"),
    "ri": ("sbuf", [128, 256], "int32"), "pint": ("sbuf", [128, 4], "int32"), "pf": ("sbuf", [128, 4], "float32"),
    "icol2": ("sbuf", [128, 256], "float32"), "gcol2": ("sbuf", [128, 256], "float32"),
    "blk": ("sbuf", [128, 128], "float32"), "mask": ("sbuf", [128, 128], "float32"),
    "m2": ("sbuf", [128, 256], "bfloat16"), "mq": ("sbuf", [128, 128], "bfloat16"), "mx": ("sbuf", [128, 128], "bfloat16"),
    "i2": ("sbuf", [128, 128], "float16"), "ni": ("sbuf", [128, 128], "float16"), "c8": ("sbuf", [128, 128], "float16"),
    "iw": ("sbuf", [128, 17, 128], "bfloat16"), "bo": ("sbuf", [128, 128], "float16"), "tri": ("sbuf", [128, 128], "float16"),
    "pos": ("sbuf", [128, 256], "float16"), "gs": ("sbuf", [128, 3, 8], "bfloat16"), "gs16": ("sbuf", [128, 8], "float16"),
    "kc": ("sbuf", [128, 128], "float16"), "cl": ("sbuf", [128, 16], "uint16"), "dumt": ("sbuf", [128, 16], "float32"),
    "nf": ("sbuf", [128, 2, 16], "float16"), "kk": ("sbuf", [128, 8], "float32"),
    "r0c": ("sbuf", [128, 2, 128], "float16"), "rl": ("sbuf", [128, 8, 128], "float16"), "rn": ("sbuf", [128, 10, 128], "float16"),
    "Xm": ("sbuf", [128, 256], "float16"), "XmT": ("sbuf", [128, 256], "float16"), "hexp": ("sbuf", [128, 256], "float32"),
    "Sc": ("sbuf", [128, 256], "float32"), "Ed": ("sbuf", [128, 4, 256], "bfloat16"), "hw": ("sbuf", [128, 16], "float32"),
    "ow": ("sbuf", [128, 16], "uint16"), "lw": ("sbuf", [128, 16], "uint16"), "t1": ("sbuf", [128, 2, 16], "float32"),
    "Pq": ("psum", [128, 512], "float32"), "Pw": ("psum", [128, 32, 16], "float32"),
}
for _u in "01":
    for _n in ("X", "F", "V", "X4", "W2"):
        SCRATCH[_n + "h" + _u] = ("sbuf", [128, 128], "bfloat16")
    for _n in ("q1", "q2", "q4", "q6", "HK", "RP", "S", "crow"):
        SCRATCH[_n + "h" + _u] = ("sbuf", [128, 128], "float16")
    SCRATCH["R1h" + _u] = ("sbuf", [128, 8, 16], "float16")
    for _n in ("SA", "Y", "RB"):
        SCRATCH[_n + "h" + _u] = ("sbuf", [128, 128], "float32")
    for _n in ("La", "Lb"):
        SCRATCH[_n + "h" + _u] = ("sbuf", [128, 128], "uint16")
    for _n in ("Ga", "Gb", "da", "db", "yb"):
        SCRATCH[_n + "h" + _u] = ("sbuf", [128, 2048], "bfloat16")
    for _n in ("d2", "y2"):
        SCRATCH[_n + "h" + _u] = ("sbuf", [128, 1024], "bfloat16")
    SCRATCH["Eh" + _u] = ("sbuf", [128, 8, 8, 16], "bfloat16")
    SCRATCH["rkh" + _u] = ("sbuf", [128, 4, 8], "float32")
    SCRATCH["sih" + _u] = ("sbuf", [128, 4, 8], "int32")
    SCRATCH["hmh" + _u] = ("sbuf", [128, 8], "int32")
    SCRATCH["Pn" + _u] = ("psum", [128, 16, 32], "float32")
    SCRATCH["Pd" + _u] = ("psum", [128, 512], "float32")
    SCRATCH["Pt" + _u] = ("psum", [128, 512], "float32")

DMAS = ["ldr", "ldx0", "ldx1", "ldc", "sty0", "sty1", "stc0", "stc1"]
SEMAPHORES = ["qv", "qs", "qt", "qg", "sent"] + ["arr%d" % k for k in range(8)] + DMAS


def rank_program(g, core, T, topo):
    rank = T.rank_of(core)
    if rank is None:
        return
    n_ranks = len(T.cores)
    nxt = T.cores[(rank + 1) % n_ranks]
    eng = {"v": g.vector, "s": g.scalar, "t": g.tensor, "g": g, "y": g.sync}
    ops, lastw, readers, banks = [], {}, {}, {}
    cur = [0.0]

    def add(q, fns, reads, writes, cost, sem=None, val=0, lat=0.0, deps=()):
        k = len(ops)
        need = set(deps)
        for a in reads:
            if a in lastw:
                need.add(lastw[a])
        for a in writes:
            if a in lastw:
                need.add(lastw[a])
            need.update(readers.get(a, ()))
        for a in set(a.split(":")[0] for a in list(reads) + list(writes) if a[0] == "P"):
            acc = banks.setdefault(a, [])
            need.update(i for qq, i in acc[-48:] if qq != q)
            acc.append((q, k))
        for a in reads:
            readers.setdefault(a, []).append(k)
        for a in writes:
            lastw[a] = k
            readers[a] = []
        need.discard(k)
        ops.append({"q": q, "f": fns, "need": need, "cost": cost, "sem": sem, "val": val, "lat": lat, "b": cur[0]})
        return k

    def dur(n, c=1.0):
        return CFG["vf"] + max(64.0, n * c) * 0.00083 * 1.1

    def size(ap):
        r = 1
        for s in ap.shape[1:]:
            r *= s
        return r

    def tt(out, a, b, op, c=None):
        ps = a[0][0] == "P" or b[0][0] == "P"
        n = size(out[1])
        return add("v", [lambda: g.vector.tensor_tensor(out=out[1], in0=a[1], in1=b[1], op=op)], [a[0], b[0]], [out[0]], dur(n, c or (1 if ps else 2)))

    def ts(out, a, s1, op0, s2=None, op1=None, c=1.0, extra=()):
        n = size(out[1])
        if op1 is None:
            f = lambda: g.vector.tensor_scalar(out=out[1], in0=a[1], scalar1=s1, scalar2=None, op0=op0)
        else:
            f = lambda: g.vector.tensor_scalar(out=out[1], in0=a[1], scalar1=s1, scalar2=s2, op0=op0, op1=op1)
        return add("v", [f], [a[0]] + list(extra), [out[0]], dur(n, c))

    def cp(out, a, c=1.0, extra=()):
        return add("v", [lambda: g.vector.tensor_copy(out=out[1], in_=a[1])], [a[0]] + list(extra), [out[0]], dur(size(out[1]), c))

    def scan(out, a, b, op0, op1, c=1.0):
        return add("v", [lambda: g.vector.tensor_tensor_scan(out=out[1], data0=a[1], data1=b[1], initial=0.0, op0=op0, op1=op1)],
                   [a[0], b[0]], [out[0]], dur(size(out[1]), c))

    def fill(key, ap, v):
        return add("v", [lambda: g.vector.memset(ap, v)], [], [key], dur(size(ap)))

    def act(out, a, func, bias=0.0, scale=1.0, c=1.0, extra=()):
        return add("s", [lambda: g.scalar.activation(out=out[1], in_=a[1], func=func, bias=bias, scale=scale)],
                   [a[0]] + list(extra), [out[0]], dur(size(out[1]), c))

    def mm(items, reads, writes):
        fns, cost = [], 0.04
        for o, l, r, st, sp in items:
            fns.append(lambda o=o, l=l, r=r, st=st, sp=sp: g.tensor.matmul(out=o, lhsT=l, rhs=r, start=st, stop=sp))
            cost += max(64, size(r)) * 0.00083 * 0.6
        return add("t", fns, reads, writes, cost)

    def B(name, u=None):
        nm = name if u is None else "%sh%d" % (name, u)
        return (nm, T[nm][:])

    add("y", [lambda: g.sync.dma_start(T.ri[:], T.r0[:])], [], ["ri"], 0.1, "ldr", 16, 2.5)
    add("s", [lambda: g.scalar.dma_start(T.xw[0:64, :], T.x[0:64, :])], [], ["xw"], 0.1, "ldx0", 16, 6.0)
    add("y", [lambda: g.sync.dma_start(T.xw[64:128, :], T.x[64:128, :])], [], ["xw_"], 0.1, "ldx1", 16, 6.5)
    add("y", [lambda: g.sync.dma_start(T.ci[:], T.c0[:])], [], ["ci"], 0.1, "ldc", 16, 5.5, deps=(1, 2))

    add("g", [lambda: g.iota(T.pint[:, 0:1], [[0, 1]], 0, 1)], [], ["pint"], 0.2)
    add("g", [lambda: g.iota(T.icol2[:], [[0, 16], [1, 16]], 0, 0, allow_small_or_imprecise_dtypes=True)], [], ["icol2"], 0.6)
    add("g", [lambda: g.iota(T.gcol2[:], [[1, 16], [0, 16]], 0, 0, allow_small_or_imprecise_dtypes=True)], [], ["gcol2"], 0.6)
    for u in (0, 1):
        cp(B("La", u), ("ri", T.ri[:, 128 * u:128 * u + 128]))
        ts(B("crow", u), ("ri", T.ri[:, 128 * u:128 * u + 128]), -OFF, OP.add)
    ts(("pi2a", T.pint[:, 1:2]), ("pint", T.pint[:, 0:1]), 15, OP.bitwise_and)
    ts(("pi2b", T.pint[:, 2:3]), ("pint", T.pint[:, 0:1]), 4, OP.arith_shift_right)
    cp(("pmod", T.pf[:, 0:1]), ("pi2a", T.pint[:, 1:2]))
    cp(("pdiv", T.pf[:, 1:2]), ("pi2b", T.pint[:, 2:3]))
    pmod, pdiv = T.pf[:, 0:1], T.pf[:, 1:2]
    ic, gc_ = ("icol2", T.icol2[:, 0:128]), ("gcol2", T.gcol2[:, 0:128])
    heads = ("blk", T.blk[:, 0:128:16])
    ts(B("mask"), ic, pmod, OP.is_equal, extra=["pmod"])
    ts(B("blk"), gc_, pdiv, OP.is_equal, extra=["pdiv"])
    tt(B("i2"), B("mask"), B("blk"), OP.mult)
    ts(B("ni"), B("i2"), -1.0, OP.mult)
    ts(B("c8"), ic, 0.0, OP.mult, NO, OP.add)
    ts(B("kc"), ic, 0.0, OP.mult, -64.0 / OFF, OP.add)
    cp(("gs0", T.gs[:, 0, :]), heads)
    ts(("gs1", T.gs[:, 1, :]), heads, 2.0, OP.mult)
    ts(("gs2", T.gs[:, 2, :]), heads, -1.0, OP.mult)
    cp(B("gs16"), heads)
    ts(B("m2"), B("icol2"), 0.0, OP.is_gt)
    ts(B("mq"), ic, 0.0, OP.is_gt, 0.25, OP.mult)
    cp(B("mx"), ("m2", T.m2[:, 0:128]))
    fill("mx", T.mx[:, 15:128:16], 0.0)
    cp(B("cl"), ("gcol2", T.gcol2[:, 0:256:16]))
    cp(B("bo"), B("blk"))
    ts(B("tri"), ic, pmod, OP.is_gt, extra=["pmod"])
    tt(B("tri"), B("tri"), B("blk"), OP.mult)
    ts(B("pos"), B("icol2"), pmod, OP.is_ge, OFF, OP.mult, extra=["pmod"])
    ts(B("dumt"), ("gcol2", T.gcol2[:, 0:256:16]), 16.0, OP.mult, pmod, OP.add, extra=["pmod"])
    ts(B("dumt"), B("dumt"), OFF, OP.add)
    cp(("iw0", T.iw[:, 0, :]), B("i2"))
    for d in range(1, 16):
        act(("iw%d" % d, T.iw[:, d, :]), ("iw0", T.iw[:, 0, :]), ID, 0.0, float(4 ** d))
    act(("iw16", T.iw[:, 16, :]), ("iw0", T.iw[:, 0, :]), ID, 0.0, -BIG)
    for u in (0, 1):
        P = T["Pd%d" % u]
        fill("Pd%d:D1" % u, P[:, 0:128], 0.0)
        fill("Pd%d:D2" % u, P[:, 128:256], 10000.0)
        ts(B("q6", u), ic, 0.0, OP.mult, NO, OP.add)
    fill("Pw:0", T.Pw[:, 0:8, :], 0.0)
    fill("Pw:1", T.Pw[:, 8:16, :], 0.0)
    fill("cw", T.cw[:, 2048:CW], 0.0)
    for k in range(2):
        cp(("cw", T.cw[:, 1024 * k:1024 * k + 1024]), ("ci", T.ci[:, 1024 * k:1024 * k + 1024]))
    for u in (0, 1):
        Pt = T["Pt%d" % u]
        mm([(Pt[:, 0:128], T["crowh%d" % u][:], T.i2[:], True, True)], ["crowh%d" % u, "i2"], ["Pt%d:A" % u])
        cp(("r0c%d" % u, T.r0c[:, u, :]), ("Pt%d:A" % u, Pt[:, 0:128]))

    def gather(u, st, t):
        L, G = T["L%sh%d" % (st, u)], T["G%sh%d" % (st, u)]
        kl, win = "L%sh%d" % (st, u), T.xw[:, 0:4096]
        nch, ndve = CFG["ch_" + st], CFG["gv_" + st]
        if t == 0 and st == "a":
            ndve = CFG["gv0"][u]
        for ch in range(nch):
            a, b = 128 // nch * ch, 128 // nch * (ch + 1)
            key = "G%sh%d.%d" % (st, u, ch)
            parts = []
            if ch == nch - 1 and ndve:
                parts = [("v", b - ndve, b)]
                b -= ndve
            if b > a:
                parts.append(("s", a, b))
            for q, a, b in parts:
                o, i = G[:, 16 * a:16 * b], win.indirect(L[:, a:b])
                if q == "s":
                    act((key + q, o), ("xw", i), ID, 16.0, c=CFG["gam"], extra=["xw_", kl])
                else:
                    ts((key + q, o), ("xw", i), 16.0, OP.add, c=CFG["gam"], extra=["xw_", kl])

    def dist(u, st, step):
        G = T["G%sh%d" % (st, u)]
        dn = "d2" if step == 2 else "d" + st
        absact = CFG["abs_2" if step == 2 else "abs_" + st]
        d = T["%sh%d" % (dn, u)]
        y = d if absact else T["%sh%d" % ("y2" if step == 2 else "y" + st, u)]
        nch = CFG["ch_" + st]
        w = 2048 // nch
        n = w // step
        for ch in range(nch):
            a, b = w * ch, w * ch + w
            key = "G%sh%d.%d" % (st, u, ch)
            kd, ky = "%sh%d.%d" % (dn, u, ch), "%sh%d.%d%s" % (dn, u, ch, "" if absact else "y")
            o = d[:, n * ch:n * ch + n - 1]
            add("v", [lambda o=o, a=a, b=b: g.vector.tensor_tensor_scan(out=o, data0=G[:, a:b - step:step], data1=G[:, a + step:b:step], initial=0.0, op0=OP.max, op1=OP.subtract)],
                [key + "s", key + "v"], [kd], dur(n, 0.5))
            yo = y[:, n * ch:n * ch + n - 1]
            if absact:
                act((ky, yo), (kd, o), ABS)
            else:
                ts((ky, yo), (kd, o), 0.0, OP.max, c=0.5)

    def sums(u, st, step):
        dn = "d2" if step == 2 else "d" + st
        absact = CFG["abs_2" if step == 2 else "abs_" + st]
        d = T["%sh%d" % (dn, u)]
        P = T["Pd%d" % u]
        items, wr = [], ["Pd%d:%s" % (u, "D1" if step == 1 else "D2")]
        per = 16 // step
        for p in range(7 if step == 2 else 15 if st == "a" else 14):
            if step == 2:
                o = P[:, 129 + 2 * p:256:16]
            elif p < 14:
                o = P[:, p + 1:128:16]
            else:
                o = P[:, 128:256:16]
                wr.append("Pd%d:D2" % u)
            if absact:
                items.append((o, d[:, p:128 * per:per], T.gs[:, 0, :], True, True))
            else:
                y = T["%sh%d" % ("y2" if step == 2 else "y" + st, u)]
                items.append((o, y[:, p:128 * per:per], T.gs[:, 1, :], True, False))
                items.append((o, d[:, p:128 * per:per], T.gs[:, 2, :], False, True))
        chs = range(CFG["ch_" + st])
        rd = ["gs0", "gs1", "gs2"] + ["%sh%d.%d" % (dn, u, ch) for ch in chs] + ([] if absact else ["%sh%d.%dy" % (dn, u, ch) for ch in chs])
        mm(items, rd, wr)

    def hold(u, reg, out, q, rk, r):
        P = T["Pd%d" % u]
        z = {"C": 256, "RB": 384}[reg]
        kp = "Pd%d:%s" % (u, reg)
        o = P[:, z:z + 128]
        mm([(o, T.i2[:], r, True, False), (o, T.i2[:], T.c8[:], False, False), (o, T.ni[:], q[1], False, True)], [rk, q[0], "i2", "c8", "ni"], [kp])
        scan(out, q, (kp, o), OP.add, OP.max)
        return kp, o

    def stage_a(t, u):
        Pn, Pd, Pt = T["Pn%d" % u], T["Pd%d" % u], T["Pt%d" % u]
        kn, kt, kX = "Pn%d:R" % u, "Pt%d:A" % u, "Xh%d" % u
        if t == 0:
            slot, r = "r0c%d" % u, T.r0c[:, u, :]
        else:
            slot, r = "rl%d" % (2 * (t - 1) + u), T.rl[:, 2 * (t - 1) + u, :]
            mm([(Pt[:, 0:128], r, T.i2[:], True, True)], [slot, "i2"], [kt])
            ts(B("La", u), (kt, Pt[:, 0:128]), OFF, OP.add)
        gather(u, "a", t)
        dist(u, "a", 1)
        sums(u, "a", 1)
        X = T["Xh%d" % u]
        scan(B("X", u), B("mx"), ("Pd%d:D1" % u, Pd[:, 0:128]), OP.mult, OP.max)
        ts(B("q1", u), B("X", u), TH, OP.is_le, NO, OP.mult, c=0.5)
        kp, rb = hold(u, "RB", B("HK", u), B("q1", u), slot, r)
        sm, si = T["rkh%d" % u], T["sih%d" % u]
        ks, kr = "sih%d." % u, "rkh%d." % u
        HK = T["HKh%d" % u]
        ts((ks + "q", si[:, 0, :]), (kp, Pd[:, 399:512:16]), OFF + 64.0, OP.add)
        ts((ks + "m", si[:, 1, :]), (ks + "q", si[:, 0, :]), 63, OP.bitwise_and)
        if t > 0:
            ts((kr + "b", sm[:, 2, :]), (ks + "m", si[:, 1, :]), 2048.0, OP.mult, T.kk[:, t - 1:t], OP.add, extra=["kk%d" % (t - 1)])
        else:
            ts((kr + "b", sm[:, 2, :]), (ks + "m", si[:, 1, :]), 2048.0, OP.mult)
        tt((kr + "p", sm[:, 0, :]), ("HKh%d" % u, HK[:, 14:128:16]), (ks + "q", si[:, 0, :]), OP.mult)
        tt((ks + "s", si[:, 2, :]), (kr + "p", sm[:, 0, :]), (kr + "b", sm[:, 2, :]), OP.add)
        ts((ks + "h", si[:, 3, :]), (ks + "s", si[:, 2, :]), 6, OP.arith_shift_right, 2047, OP.bitwise_and)
        act(B("RB", u), (kp, rb), ID)
        tt((kr + "xf", sm[:, 3, :]), (kX, X[:, 14:128:16]), ("Pd%d:D2" % u, Pd[:, 128:256:16]), OP.max)
        nf = ("nf%d.%d" % (t % 2, u), T.nf[:, t % 2, 8 * u:8 * u + 8])
        ts(nf, (kr + "xf", sm[:, 3, :]), TH, OP.is_le, OFF, OP.mult)
        tt(B("hm", u), (ks + "h", si[:, 3, :]), nf, OP.max)
        Xm = T.Xm[:, 128 * u:128 * u + 128]
        add("v", [lambda: g.vector.tensor_tensor(out=Xm, in0=T["hmh%d" % u][:, 0:8].indirect(T.cl[:, 0:8]), in1=T.mask[:], op=OP.mult)],
            ["hmh%d" % u, "cl", "mask"], ["Xm%d" % u], dur(128, CFG["gam"]))
        mm([(Pt[:, 0:8], Xm, T.gs16[:], True, True)], ["Xm%d" % u, "gs16"], [kt])
        ow = ("ow%d" % u, T.ow[:, 8 * u:8 * u + 8])
        cp(ow, (kt, Pt[:, 0:8]))
        ts(B("crow", u), ("cw", T.cw[:, 0:CW].indirect(ow[1])), -OFF, OP.add, c=CFG["gam"], extra=[ow[0]])
        kc, C = "Pd%d:C" % u, Pd[:, 256:384]
        mm([(C, T["crowh%d" % u][:], T.i2[:], True, False), (C, T.i2[:], T["q1h%d" % u][:], False, True)], ["crowh%d" % u, "q1h%d" % u, "i2"], [kc])
        tt(B("R1", u), B("RB", u), (kc, C), OP.max)
        R1, E = T["R1h%d" % u], T["Eh%d" % u]
        mm([(Pn[:, 0:8, 0:16], T.i2[:], R1[:], True, True), (Pn[:, 0:8, 16:24], T.i2[:], R1[:, :, 0:8], True, True)], ["R1h%d" % u, "i2"], [kn])
        kw, W = "Pw:%d" % u, T.Pw[:, 8 * u:8 * u + 8, :]
        for d in range(1, 9):
            n = 16 if d < 8 else 8
            ke, e = "Eh%d.%d" % (u, d), 16 - d
            tt((ke, E[:, d - 1, :, 0:n]), ("R1h%d" % u, R1[:, :, 0:n]), (kn, Pn[:, 0:8, d:d + n]), OP.is_equal)
            its = [(T.Pw[:, 8 * u:8 * u + 8, 1:e + 1], T.iw[:, d, :], E[:, d - 1, :, 0:e], d == 1, d == 8)]
            if d < 8:
                its.append((T.Pw[:, 8 * u:8 * u + 8, 1:d + 1], T.iw[:, e, :], E[:, d - 1, :, e:16], False, False))
            mm(its, [ke, "iw%d" % d, "iw%d" % e], [kw])
        cp(B("W2", u), (kw, W))
        scan(B("F", u), ("m2", T.m2[:, 0:128]), B("W2", u), OP.mult, OP.max, 0.5)
        mm([(C, T.iw[:, 0, :], T["W2h%d" % u][:], True, False), (Pd[:, 257:384], T.iw[:, 16, :], T["Fh%d" % u][:, 0:127], False, True)],
           ["W2h%d" % u, "Fh%d" % u, "iw0", "iw16"], [kc])
        scan(B("V", u), B("mq"), (kc, C), OP.mult, OP.max)
        ts(B("q2", u), B("V", u), 4.0, OP.is_lt, NO, OP.mult, c=0.5)
        hold(u, "RB", B("RP", u), B("q2", u), "R1h%d" % u, R1[:])
        mm([(Pt[:, 0:128], T["RPh%d" % u][:], T.i2[:], True, True)], ["RPh%d" % u, "i2"], [kt])
        ts(B("Lb", u), (kt, Pt[:, 0:128]), OFF, OP.add)

    def stage_b(t, u):
        Pd, Pt = T["Pd%d" % u], T["Pt%d" % u]
        kt = "Pt%d:A" % u
        RP = T["RPh%d" % u][:]
        gather(u, "b", t)
        dist(u, "b", 2)
        dist(u, "b", 1)
        sums(u, "b", 2)
        ts(("q6h%d" % u, T["q6h%d" % u][:, 1:128:2]), ("Pd%d:D2" % u, Pd[:, 129:256:2]), TH, OP.is_gt, NO, OP.mult)
        k = 2 * t + u
        slot, rn = "rn%d" % k, T.rn[:, k, :]
        hold(u, "RB", (slot, rn), B("q6", u), "RPh%d" % u, RP)
        if t < ROUNDS - 1:
            rid, pid, _s = topo.addr(nxt)
            m = 0
            for e in topo.engines(core, nxt)[:NENG]:
                m |= 1 << e
            sd = add("g", [lambda: g.remote_dma(out_ap=T.rl[:, k, :], in_ap=rn, remote_sem=T.sem["arr%d" % k], local_sem=T.sem.sent, pid=pid, routing_id=rid, dma_engine_mask=m)],
                     [slot], [], 0.3, "none", 0, 1.7)
            add(None, [], [], ["rl%d" % k], 0.0, "arr%d" % k, NENG, 0.0, deps=[sd])
        sums(u, "b", 1)
        scan(B("X4", u), B("mx"), ("Pd%d:D1" % u, Pd[:, 0:128]), OP.mult, OP.max)
        ts(B("q4", u), B("X4", u), TH, OP.is_le, NO, OP.mult, c=0.5)
        hold(u, "C", B("S", u), B("q4", u), "RPh%d" % u, RP)
        mm([(Pt[:, 0:128], T["Sh%d" % u][:], T.i2[:], True, True)], ["Sh%d" % u, "i2"], [kt])
        act(B("SA", u), (kt, Pt[:, 0:128]), ID, OFF)
        if t == ROUNDS - 1:
            mm([(Pt[:, 128:256], rn, T.i2[:], True, True)], [slot, "i2"], ["Pt%d:Y" % u])
            act(B("Y", u), ("Pt%d:Y" % u, Pt[:, 128:256]), ID, OFF)
            add("y", [lambda: g.sync.dma_start(T.yr[:, 128 * u:128 * u + 128], T["Yh%d" % u][:])], ["Yh%d" % u], [], 0.1, "sty%d" % u, 16, 2.0)

    def count(t):
        f = T.nf[:, t % 2, :]
        mm([(T.Pt1[:, 256:272], T.kc[:], f, True, True)], ["nf%d.0" % (t % 2), "nf%d.1" % (t % 2), "kc"], ["Pt1:K"])
        add("v", [lambda: g.vector.tensor_reduce(out=T.kk[:, t:t + 1], in_=T.Pt1[:, 256:272], axis=AxisListType.X, op=OP.add)], ["Pt1:K"], ["kk%d" % t], dur(16))

    def winners():
        q = T.Pq
        mm([(q[:, 128 * u:128 * u + 128], T.Xm[:, 128 * u:128 * u + 128], T.i2[:], True, True) for u in (0, 1)], ["Xm0", "Xm1", "i2"], ["Pq:L"])
        cp(B("XmT"), ("Pq:L", q[:, 0:256]))
        cp(B("hw"), ("ow0", T.ow[:]), extra=["ow1"])
        act(B("hexp"), ("hw", T.hw[:, 0:16].indirect(T.cl[:, 0:16])), ID, c=CFG["gam"], extra=["cl"])
        mm([(q[:, 0:256], T.bo[:], T.XmT[:], True, True)], ["XmT", "bo"], ["Pq:L"])
        mm([(q[:, 256:512], T.tri[:], T.XmT[:], True, False), (q[:, 256:512], T.i2[:], T.pos[:], False, True)], ["XmT", "tri", "i2", "pos"], ["Pq:R"])
        for k in range(4):
            w = 256 - 16 * k
            a = ("Pq:R", q[:, 256:512]) if k == 0 else ("Pq:L", q[:, 0:w])
            tt(("Ed%d" % k, T.Ed[:, k, 0:w]), ("hexp", T.hexp[:, 16 * k:256]), a, OP.is_equal)
        mm([(q[:, 16 * k:256], T.iw[:, 6, :], T.Ed[:, k, 0:256 - 16 * k], k == 0, k == 3) for k in range(4)],
           ["Ed%d" % k for k in range(4)] + ["iw6"], ["Pq:L"])
        scan(B("Sc"), B("m2"), ("Pq:L", q[:, 0:256]), OP.mult, OP.max)
        tt(("t1a", T.t1[:, 0, :]), ("Sc", T.Sc[:, 15:256:16]), B("dumt"), OP.min)
        tt(("t1b", T.t1[:, 1, :]), ("t1a", T.t1[:, 0, :]), B("hw"), OP.max)
        cp(B("lw"), ("t1b", T.t1[:, 1, :]))

    def scatter(u):
        for k in (1, 0):
            o = T.cw[:, 0:CW].indirect(T.lw[:, 8 * u + 4 * k:8 * u + 4 * k + 4])
            add("v", [lambda o=o, k=k: g.vector.tensor_copy(out=o, in_=T["SAh%d" % u][:, 64 * k:64 * k + 64])], ["SAh%d" % u, "lw"], ["cw"], dur(64, 3.5))

    for t in range(ROUNDS):
        cur[0] = CFG["b0"]
        stage_a(t, 0)
        cur[0] = 0.0
        stage_a(t, 1)
        if t < ROUNDS - 1:
            count(t)
        winners()
        cur[0] = CFG["b0"] + CFG["bb"]
        stage_b(t, 0)
        cur[0] = CFG["bb"]
        stage_b(t, 1)
        cur[0] = CFG["bs"]
        scatter(1)
        scatter(0)
    add("s", [lambda: g.scalar.dma_start(T.yc[0:64, :], T.cw[0:64, 0:2048])], ["cw"], [], 0.1, "stc0", 16, 5.0)
    add("y", [lambda: g.sync.dma_start(T.yc[64:128, :], T.cw[64:128, 0:2048])], ["cw"], [], 0.1, "stc1", 16, 5.0)

    n = len(ops)
    users = [[] for _ in range(n)]
    for k, o in enumerate(ops):
        for d in o["need"]:
            users[d].append(k)
    way = [0.0] * n
    for k in range(n - 1, -1, -1):
        o = ops[k]
        way[k] = o["cost"] + o["lat"] + CFG["wake"] + max([way[j] for j in users[k]] or [0.0])
    way = [w + o["b"] for w, o in zip(way, ops)]
    left = [len(o["need"]) for o in ops]
    at = [0.0] * n
    free = {q: 0.0 for q in ("v", "s", "t", "g", "y", None)}
    pool = [k for k in range(n) if left[k] == 0]
    order = []
    while pool:
        best, bs, bst = None, None, 0.0
        for k in pool:
            o = ops[k]
            st = max(free[o["q"]] if o["q"] else 0.0, at[k])
            key = (st - CFG["ww"] * way[k], -way[k])
            if bs is None or key < bs:
                best, bs, bst = k, key, st
        pool.remove(best)
        o = ops[best]
        st = bst
        if o["q"]:
            free[o["q"]] = st + o["cost"]
        done = st + o["cost"] + o["lat"]
        order.append(best)
        for j in users[best]:
            lag = 0.0 if ops[j]["q"] == o["q"] == "t" else CFG["wake"]
            at[j] = max(at[j], done + lag)
            left[j] -= 1
            if left[j] == 0:
                pool.append(j)
    CFG["ms"] = max(free.values())

    total = {"qv": 0, "qs": 0, "qt": 0, "qg": 0}
    known = {q: {} for q in eng}
    for k in order:
        o = ops[k]
        q = o["q"]
        if q is None:
            continue
        want = {}
        for d in o["need"]:
            p = ops[d]
            if p["sem"] == "none" or (p["q"] == q and q == "t"):
                continue
            want[p["sem"]] = max(want.get(p["sem"], 0), p["val"])
        for s in sorted(want):
            if known[q].get(s, 0) < want[s]:
                known[q][s] = want[s]
                eng[q].wait_ge(T.sem[s], want[s])
        fresh = o["sem"] is None
        for f in o["f"]:
            ins = f()
            if fresh:
                o["sem"] = "q" + q
                total["q" + q] += 1
                o["val"] = total["q" + q]
                ins.then_inc(T.sem["q" + q], 1)
            elif o["sem"] != "none":
                ins.then_inc(T.sem[o["sem"]], 16)
    for s in sorted(total):
        g.wait_ge(T.sem[s], total[s])
    for s in DMAS:
        g.wait_ge(T.sem[s], 16)
    g.wait_ge(T.sem.sent, 2 * (ROUNDS - 1) * NENG)
